import numpy as np
import ml_dtypes


def mxq(x, axis, fmt="e4m3"):
    dtype, down = {"e4m3": (ml_dtypes.float8_e4m3fn, 7), "e5m2": (ml_dtypes.float8_e5m2, 14)}[fmt]
    v = np.moveaxis(np.asarray(x, np.float32).astype(ml_dtypes.bfloat16).astype(np.float64), axis, -1)
    blocks = v.reshape(v.shape[:-1] + (-1, 32))
    amax = np.abs(blocks).max(-1, keepdims=True)
    byte = np.maximum(np.where(amax > 0, np.frexp(amax)[1] - 1 + 127, 0) - down, 1)
    scale = np.exp2(byte - 127.0)
    codes = (blocks / scale).astype(np.float32).astype(dtype).astype(np.float64)
    return np.moveaxis((codes * scale).reshape(v.shape), -1, axis)


WIDE = False


def mx_kscale(k):
    if not WIDE:
        return np.ones(k)
    levels = np.array([10, -10, 5, -5, 0])
    if k % 512:
        return np.exp2(np.random.permutation(np.resize(levels, k // 32))).repeat(32)
    a = np.empty((k // 512, 16))
    for p in range(k // 512):
        a[p, :8] = np.random.permutation(np.resize(levels, 8))
        for g in range(8):
            far = levels[np.abs(levels - a[p, g]) >= 10]
            a[p, g + 8] = far[np.random.randint(len(far))]
    return np.exp2(a.ravel()).repeat(32)


def f64(x):
    return np.asarray(x).astype(np.float64)


def striped(idx):
    return np.tile(idx.reshape(-1, 16).T, (8, 1)).astype(np.uint16)


def unstriped(offs):
    return offs[:16].T.reshape(-1).astype(np.int64)


def striped8(idx):
    return np.concatenate([x.reshape(-1, 16).T for x in idx]).astype(np.uint16)


def runs(offs, k):
    lists = np.stack([offs[16 * r : 16 * r + 16].T.reshape(-1) for r in range(8)]).astype(np.int64)
    return lists[np.arange(k) % 512 // 64]


def pack_weight(w):
    k, n = w.shape
    w = f64(np.asarray(w, np.float32).astype(ml_dtypes.bfloat16)).reshape(k // 32, 32, n)
    amax = np.abs(w).max(1)
    byte = np.clip(np.where(amax > 0, np.frexp(amax)[1] - 1 + 127 - 7, 1), 1, 254)
    scaled = (w * np.exp2(127.0 - byte)[:, None, :]).reshape(k, n).astype(np.float32)
    words = np.ascontiguousarray(scaled.reshape(k // 512, 128, 4, n).transpose(0, 1, 3, 2)).astype(ml_dtypes.float8_e4m3fn).view(np.uint8)
    return words, np.ascontiguousarray(byte.astype(np.uint8).reshape(k // 512, 16, n))


def unpack_weight(words, scales):
    g, p, n, _ = words.shape
    vals = np.ascontiguousarray(words).view(ml_dtypes.float8_e4m3fn).astype(np.float64) * np.repeat(np.exp2(scales.astype(np.float64) - 127.0), 8, axis=1)[..., None]
    return vals.transpose(0, 1, 3, 2).reshape(g * 512, n)


E2M1 = np.array([0.0, 0.5, 1.0, 1.5, 2.0, 3.0, 4.0, 6.0, -0.0, -0.5, -1.0, -1.5, -2.0, -3.0, -4.0, -6.0])


def pack_fp4(w):
    k, n = w.shape
    w = f64(np.asarray(w, np.float32).astype(ml_dtypes.bfloat16)).reshape(k // 32, 32, n)
    amax = np.abs(w).max(1)
    mant, ex = np.frexp(amax / 6.0)
    byte = np.clip(np.where(amax > 0, np.where(mant > 0.5, ex, ex - 1) + 127, 1), 1, 254)
    scaled = (w * np.exp2(127.0 - byte)[:, None, :]).reshape(k, n).astype(np.float32)
    c = np.ascontiguousarray(scaled.reshape(k // 512, 128, 4, n).transpose(0, 1, 3, 2)).astype(ml_dtypes.float4_e2m1fn).view(np.uint8) & 0xF
    words = (c[..., 0::2] | (c[..., 1::2] << 4)).reshape(k // 512, 128, 2 * n)
    return np.ascontiguousarray(words), np.ascontiguousarray(byte.astype(np.uint8).reshape(k // 512, 16, n))


def unpack_fp4(words, scales):
    g, _, n = scales.shape
    words = np.ascontiguousarray(words).reshape(g, 128, n, 2)
    nib = np.empty((g, 128, n, 4), np.uint8)
    nib[..., 0::2] = words & 0xF
    nib[..., 1::2] = words >> 4
    vals = E2M1[nib] * np.repeat(np.exp2(scales.astype(np.float64) - 127.0), 8, axis=1)[..., None]
    return vals.transpose(0, 1, 3, 2).reshape(g * 512, n)


def sigmoid(v):
    return 1.0 / (1.0 + np.exp(-np.maximum(v, -700.0)))

def planes(y):
    n, m = y.shape
    v = y.astype(np.float32).astype(ml_dtypes.bfloat16).astype(np.float64).reshape(n // 32, 32, m)
    top = np.abs(v).max(1)
    byte = np.clip(np.where(top > 0, np.frexp(top)[1] - 1 + 127 - 7, 1), 1, 254)
    codes = (v * np.exp2(127.0 - byte)[:, None, :]).reshape(n, m).astype(np.float32).astype(ml_dtypes.float8_e4m3fn).view(np.uint8)
    words = codes.reshape(n // 512, 128, 4, m).transpose(0, 1, 3, 2)
    return np.ascontiguousarray(words), np.ascontiguousarray(byte.astype(np.uint8).reshape(n // 512, 16, m))


K, T, S, H, J = 512, 2048, 512, 512, 512


def setup_inputs():
    n = np.random.standard_normal
    s = mx_kscale(K)[:, None]
    u = mx_kscale(H)
    packed_xT = pack_weight(n((K, T)) * s)
    packed_w1 = pack_fp4(n((K, H)) / np.sqrt(K) / s)
    packed_w2 = pack_fp4(n((H, H)) / np.sqrt(H) / u[:, None])
    return {
        "x_words": packed_xT[0],
        "x_scales": packed_xT[1],
        "w1_words": packed_w1[0],
        "w1_scales": packed_w1[1],
        "tab": n((H, J)).astype(np.float32),
        "gn": (np.random.uniform(0.5, 1.5, (H, 1)) * u[:, None]).astype(np.float32),
        "w2_words": packed_w2[0],
        "w2_scales": packed_w2[1],
        "offs": striped(np.random.permutation(T)[:S]),
        "n1": striped8(np.stack([np.random.permutation(S) for _ in range(8)])),
        "n2": striped8(np.random.randint(0, J, (8, S))),
        "n3": striped8(np.stack([np.random.permutation(S) for _ in range(8)])),
        "n4": striped8(np.stack([np.random.permutation(S) for _ in range(8)])),
        "n5": striped8(np.stack([np.random.permutation(S) for _ in range(8)])),
    }


def reference(x_words, x_scales, w1_words, w1_scales, tab, gn, w2_words, w2_scales, offs, n1, n2, n3, n4, n5):
    xq = unpack_weight(x_words, x_scales)[:, unstriped(offs)]
    y = unpack_fp4(w1_words, w1_scales).T @ xq
    pa = y[np.arange(H)[:, None], runs(n1, H)]
    z = f64(gn) * ((2.0 * (y * pa)) / ((y) ** 2 + (pa) ** 2 + 0.5))
    w2q = unpack_fp4(w2_words, w2_scales)
    a = w2q.T @ mxq(z, 0, "e4m3")
    z2 = f64(gn) * (np.abs(y - (y[np.arange(H)[:, None], runs(n3, H)]) - (f64(tab)[np.arange(H)[:, None], runs(n2, H)])))
    b = w2q.T @ mxq(z2, 0, "e4m3")
    out_0 = a * (sigmoid(b[np.arange(H)[:, None], runs(n5, H)])) - (0.5 * (a[np.arange(H)[:, None], runs(n4, H)]))
    return (out_0,) + planes(out_0)

@@ -1,0 +1,222 @@
+from contextlib import ExitStack
+
+import concourse.mybir as mybir
+
+F32 = mybir.dt.float32
+BF16 = mybir.dt.bfloat16
+I32 = mybir.dt.int32
+U32 = mybir.dt.uint32
+U16 = mybir.dt.uint16
+U8 = mybir.dt.uint8
+FP8X4 = mybir.dt.float8_e4m3fn_x4
+FP4X4 = mybir.dt.float4_e2m1fn_x4
+ALU = mybir.AluOpType
+ACT = mybir.ActivationFunctionType
+
+P = 128
+PACK = 4
+T = 2048
+S = 512
+H = 512
+HALF = S // 2
+FLOPS = 3 * 2 * 512 * 512 * 512
+
+
+def tile_picked_tiegatebharmkindd_none_po_kernel(
+    tc, x_words, x_scales, w1_words, w1_scales, tab, gn, w2_words, w2_scales, offs, n1, n2, n3, n4, n5, out_0, out_1, out_2
+):
+    nc = tc.nc
+    with ExitStack() as ctx:
+        lists = ctx.enter_context(tc.tile_pool(name="lists", bufs=1))
+        keep = ctx.enter_context(tc.tile_pool(name="keep", bufs=1))
+        psum = ctx.enter_context(tc.psum_pool(name="psum", bufs=1))
+
+        def load_list(src, name):
+            tile = lists.tile([P, S // 16], U16, name=name)
+            nc.sync.dma_start(tile[:], src)
+            return tile
+
+        def half_of(lst, h):
+            return lst[:, h * (HALF // 16) : (h + 1) * (HALF // 16)]
+
+        def cols(h):
+            return slice(h * HALF, (h + 1) * HALF)
+
+        def load_scale_rows(tile, src):
+            for q in range(4):
+                nc.sync.dma_start(tile[32 * q : 32 * q + 4, :].bitcast(I32), src[0, 4 * q : 4 * q + 4, :].bitcast(I32))
+
+        def planes(name, dtype=F32):
+            return keep.tile([P, PACK, S], dtype, name=name, align_bytes=64)
+
+        def rows(name):
+            return [keep.tile([P, S], F32, name="%s%d" % (name, t), align_bytes=64) for t in range(PACK)]
+
+        xs_raw = keep.tile([P, T], U8, name="xs_raw", align_bytes=64)
+        w1s_raw = keep.tile([P, H], U8, name="w1s_raw", align_bytes=64)
+        w2s_raw = keep.tile([P, H], U8, name="w2s_raw", align_bytes=64)
+        for tile in (xs_raw, w1s_raw, w2s_raw):
+            nc.vector.memset(tile[:].bitcast(I32), 0)
+
+        xw_raw = keep.tile([P, T], U32, name="xw_raw", align_bytes=64)
+        w1w_raw = keep.tile([P, 2 * H], U8, name="w1w_raw", align_bytes=64)
+        w2w_raw = keep.tile([P, 2 * H], U8, name="w2w_raw", align_bytes=64)
+        tab_t = rows("tab")
+        gain = keep.tile([P, PACK], F32, name="gain")
+
+        load_scale_rows(xs_raw, x_scales)
+        offs_t = load_list(offs, "offs_t")
+        nc.sync.dma_start(w1w_raw[:].bitcast(I32), w1_words[0].bitcast(I32))
+        nc.sync.dma_start(xw_raw[:].bitcast(I32), x_words[0].rearrange("p c r -> p (c r)").bitcast(I32))
+        load_scale_rows(w1s_raw, w1_scales)
+        n2_t = load_list(n2, "n2_t")
+        tab_rows = tab.rearrange("(p t) j -> t p j", t=PACK)
+        nc.sync.dma_start(tab_t[0][:], tab_rows[0])
+        n1_t = load_list(n1, "n1_t")
+        nc.sync.dma_start(gain[:], gn.rearrange("(p t) o -> p (t o)", t=PACK))
+        for t in range(1, PACK):
+            nc.sync.dma_start(tab_t[t][:], tab_rows[t])
+        n3_t = load_list(n3, "n3_t")
+        nc.sync.dma_start(w2w_raw[:].bitcast(I32), w2_words[0].bitcast(I32))
+        load_scale_rows(w2s_raw, w2_scales)
+        n4_t = load_list(n4, "n4_t")
+        n5_t = load_list(n5, "n5_t")
+
+        def deal(words_raw, scales_raw, name):
+            words = keep.tile([P, 2 * H], U8, name=name + "_words", align_bytes=64)
+            scales = keep.tile([P, H], U8, name=name + "_scales", align_bytes=64)
+            nc.scalar.copy(
+                words[:].bitcast(U16).rearrange("p (t m) -> p t m", t=PACK),
+                words_raw[:].bitcast(U16).rearrange("p (m t) -> p t m", t=PACK),
+            )
+            nc.gpsimd.tensor_copy(
+                scales[:].rearrange("p (t m) -> p t m", t=PACK),
+                scales_raw[:].rearrange("p (m t) -> p t m", t=PACK),
+            )
+            return words, scales
+
+        def product(weights, codes, scales, tag):
+            words, wscales = weights
+            banks = []
+            for t in range(PACK):
+                bank = psum.tile([P, S], F32, name="%s%d" % (tag, t))
+                nc.tensor.matmul_mx(
+                    out=bank[:],
+                    lhsT=words[:, 2 * P * t : 2 * P * (t + 1)].bitcast(FP4X4),
+                    lhsT_scale=wscales[:, P * t : P * (t + 1)],
+                    rhs=codes[:].bitcast(FP8X4),
+                    rhs_scale=scales[:],
+                    start=True,
+                    stop=True,
+                )
+                banks.append(bank)
+            return banks
+
+        def weave(dst, src, copy):
+            copy(dst.rearrange("p (c i) t -> p c t i", i=4), src.rearrange("p t (c i) -> p c t i", i=4))
+
+        def quantise(flat, name):
+            woven = keep.tile([P, S, PACK], BF16, name=name + "_woven", align_bytes=64)
+            codes = keep.tile([P, S], U32, name=name + "_codes", align_bytes=64)
+            scales = keep.tile([P, S], U8, name=name + "_scales", align_bytes=64)
+            weave(woven[:], flat[:], nc.vector.tensor_copy)
+            nc.vector.quantize_mx(codes[:].bitcast(FP8X4), scales[:], woven[:].rearrange("p c t -> p (c t)"))
+            return codes, scales
+
+        w1 = deal(w1w_raw, w1s_raw, "w1")
+        xs = keep.tile([P, S], U8, name="xs", align_bytes=64)
+        xw = keep.tile([P, S], U32, name="xw", align_bytes=64)
+        nc.vector.tensor_copy(xs[:], xs_raw[:].indirect(offs_t[:]))
+        nc.vector.tensor_copy(xw[:], xw_raw[:].indirect(offs_t[:]))
+        y_banks = product(w1, xw, xs, "ya")
+        w2 = deal(w2w_raw, w2s_raw, "w2")
+
+        tab_g = planes("tab_g")
+        for t in range(PACK):
+            for h in range(2):
+                nc.scalar.activation(tab_g[:, t, cols(h)], tab_t[t][:].indirect(half_of(n2_t, h)), ACT.Copy)
+
+        gain2 = keep.tile([P, PACK], F32, name="gain2")
+        nc.vector.tensor_scalar(gain2[:], gain[:], 2.0, None, ALU.mult)
+
+        y = rows("y")
+        for t in range(PACK):
+            if t in ():
+                nc.scalar.copy(y[t][:], y_banks[t][:])
+            else:
+                nc.vector.tensor_copy(y[t][:], y_banks[t][:])
+
+        both, diff, size = (planes(n) for n in ("both", "diff", "size"))
+        z2 = planes("z2", BF16)
+        for t in range(PACK):
+            for h in range(2):
+                nc.vector.tensor_tensor(both[:, t, cols(h)], y[t][:].indirect(half_of(n3_t, h)), tab_g[:, t, cols(h)], ALU.add)
+            nc.vector.tensor_tensor(diff[:, t, :], y[t][:], both[:, t, :], ALU.subtract)
+            nc.scalar.activation(size[:, t, :], diff[:, t, :], ACT.Abs)
+        for t in range(PACK):
+            nc.vector.tensor_scalar(z2[:, t, :], size[:, t, :], gain[:, t : t + 1], None, ALU.mult)
+        z2_codes, z2_scales = quantise(z2, "z2")
+        b_banks = product(w2, z2_codes, z2_scales, "b")
+
+        pa, y_sq, pa_sq, den, recip, num = (planes(n) for n in ("pa", "y_sq", "pa_sq", "den", "recip", "num"))
+        root = [keep.tile([P, S], F32, name="root%d" % t, tag="root_or_b%d" % t, align_bytes=64) for t in range(PACK)]
+        z = planes("z", BF16)
+        for t in range(PACK):
+            for h in range(2):
+                if t in (0,1,2):
+                    nc.scalar.activation(pa[:, t, cols(h)], y[t][:].indirect(half_of(n1_t, h)), ACT.Copy)
+                else:
+                    nc.vector.tensor_copy(pa[:, t, cols(h)], y[t][:].indirect(half_of(n1_t, h)))
+            if t in ():
+                nc.vector.tensor_tensor(y_sq[:, t, :], y[t][:], y[t][:], ALU.mult)
+            elif t in ():
+                nc.gpsimd.tensor_tensor(y_sq[:, t, :], y[t][:], y[t][:], ALU.mult)
+            else:
+                nc.scalar.activation(y_sq[:, t, :], y[t][:], ACT.Square)
+            nc.scalar.activation(pa_sq[:, t, :], pa[:, t, :], ACT.Square)
+        for t in range(PACK):
+            nc.vector.scalar_tensor_tensor(den[:, t, :], pa_sq[:, t, :], 0.5, y_sq[:, t, :], ALU.add, ALU.add)
+        for t in range(PACK):
+            nc.scalar.activation(root[t][:], den[:, t, :], ACT.Abs_reciprocal_sqrt)
+            nc.scalar.activation(recip[:, t, :], root[t][:], ACT.Square)
+        for t in range(PACK):
+            nc.vector.scalar_tensor_tensor(num[:, t, :], pa[:, t, :], gain2[:, t : t + 1], y[t][:], ALU.mult, ALU.mult)
+            nc.vector.tensor_tensor(z[:, t, :], num[:, t, :], recip[:, t, :], ALU.mult)
+        z_codes, z_scales = quantise(z, "z")
+        a_banks = product(w2, z_codes, z_scales, "ya")
+
+        b = [keep.tile([P, S], F32, name="b%d" % t, tag="root_or_b%d" % (PACK - 1 - t), align_bytes=64) for t in range(PACK)]
+        neg_half_a = rows("neg_half_a")
+        gate, gated, result = (planes(n) for n in ("gate", "gated", "result"))
+        out_rows = out_0.rearrange("(p t) j -> t p j", t=PACK)
+        fetched = planes("fetched")
+        for t in range(PACK):
+            if t in ():
+                nc.scalar.copy(b[t][:], b_banks[t][:])
+            else:
+                nc.vector.tensor_copy(b[t][:], b_banks[t][:])
+        for t in range(PACK):
+            nc.scalar.activation(neg_half_a[t][:], a_banks[t][:], ACT.Copy, scale=-0.5)
+            for h in range(2):
+                nc.scalar.activation(gate[:, t, cols(h)], b[t][:].indirect(half_of(n5_t, h)), ACT.Sigmoid)
+            nc.vector.scalar_tensor_tensor(gated[:, t, :], gate[:, t, :], -2.0, neg_half_a[t][:], ALU.mult, ALU.mult)
+            if t in (3,):
+                for h in range(2):
+                    nc.scalar.activation(fetched[:, t, cols(h)], neg_half_a[t][:].indirect(half_of(n4_t, h)), ACT.Copy)
+                nc.vector.tensor_tensor(result[:, t, :], fetched[:, t, :], gated[:, t, :], ALU.add)
+            else:
+                for h in range(2):
+                    nc.vector.tensor_tensor(result[:, t, cols(h)], neg_half_a[t][:].indirect(half_of(n4_t, h)), gated[:, t, cols(h)], ALU.add)
+            nc.sync.dma_start(out_rows[t], result[:, t, :])
+
+        out_codes = keep.tile([P, S], U32, name="out_codes", align_bytes=64)
+        out_scales = keep.tile([P, S], U8, name="out_scales", align_bytes=64)
+        out_words = out_1[0].rearrange("p c r -> p (c r)").bitcast(I32)
+        split = 320
+        woven = keep.tile([P, S, PACK], BF16, name="out_woven", align_bytes=64)
+        weave(woven[:, :split, :], result[:, :, :split], nc.vector.tensor_copy)
+        weave(woven[:, split:, :], result[:, :, split:], nc.scalar.copy)
+        nc.vector.quantize_mx(out_codes[:].bitcast(FP8X4), out_scales[:], woven[:].rearrange("p c t -> p (c t)"))
+        nc.sync.dma_start(out_words, out_codes[:].bitcast(I32))
+        for q in range(4):
+            nc.scalar.dma_start(out_2[0, 4 * q : 4 * q + 4, :].bitcast(I32), out_scales[32 * q : 32 * q + 4, :].bitcast(I32))

@@ -1,6 +1,7 @@
 from contextlib import ExitStack
 
 import concourse.mybir as mybir
+from concourse.masks import make_identity
 
 F32 = mybir.dt.float32
 BF16 = mybir.dt.bfloat16
@@ -64,23 +65,26 @@ def tile_picked_tiegatebharmkindd_none_po_kernel(
         tab_t = rows("tab")
         gain = keep.tile([P, PACK], F32, name="gain")
 
-        load_scale_rows(xs_raw, x_scales)
+        x_rows = x_words[0].rearrange("p c r -> p (c r)").bitcast(I32)
+        tab_rows = tab.rearrange("(p t) j -> t p j", t=PACK)
         offs_t = load_list(offs, "offs_t")
         nc.sync.dma_start(w1w_raw[:].bitcast(I32), w1_words[0].bitcast(I32))
-        nc.sync.dma_start(xw_raw[:].bitcast(I32), x_words[0].rearrange("p c r -> p (c r)").bitcast(I32))
-        load_scale_rows(w1s_raw, w1_scales)
+        nc.sync.dma_start(xw_raw[:, : T // 2].bitcast(I32), x_rows[:, : T // 2])
         n2_t = load_list(n2, "n2_t")
-        tab_rows = tab.rearrange("(p t) j -> t p j", t=PACK)
         nc.sync.dma_start(tab_t[0][:], tab_rows[0])
-        n1_t = load_list(n1, "n1_t")
-        nc.sync.dma_start(gain[:], gn.rearrange("(p t) o -> p (t o)", t=PACK))
-        for t in range(1, PACK):
-            nc.sync.dma_start(tab_t[t][:], tab_rows[t])
+        load_scale_rows(xs_raw, x_scales)
+        nc.sync.dma_start(xw_raw[:, T // 2 :].bitcast(I32), x_rows[:, T // 2 :])
+        load_scale_rows(w1s_raw, w1_scales)
+        nc.sync.dma_start(tab_t[1][:], tab_rows[1])
+        nc.sync.dma_start(tab_t[2][:], tab_rows[2])
+        nc.sync.dma_start(tab_t[3][:], tab_rows[3])
         n3_t = load_list(n3, "n3_t")
         nc.sync.dma_start(w2w_raw[:].bitcast(I32), w2_words[0].bitcast(I32))
+        n1_t = load_list(n1, "n1_t")
+        nc.sync.dma_start(gain[:], gn.rearrange("(p t) o -> p (t o)", t=PACK))
         load_scale_rows(w2s_raw, w2_scales)
-        n4_t = load_list(n4, "n4_t")
         n5_t = load_list(n5, "n5_t")
+        n4_t = load_list(n4, "n4_t")
 
         def deal(words_raw, scales_raw, name):
             words = keep.tile([P, 2 * H], U8, name=name + "_words", align_bytes=64)
@@ -95,11 +99,11 @@ def tile_picked_tiegatebharmkindd_none_po_kernel(
             )
             return words, scales
 
-        def product(weights, codes, scales, tag):
+        def product(weights, codes, scales, name, first):
             words, wscales = weights
             banks = []
             for t in range(PACK):
-                bank = psum.tile([P, S], F32, name="%s%d" % (tag, t))
+                bank = psum.tile([P, S], F32, name="%s%d" % (name, t), tag="bank%d" % (first + t))
                 nc.tensor.matmul_mx(
                     out=bank[:],
                     lhsT=words[:, 2 * P * t : 2 * P * (t + 1)].bitcast(FP4X4),
@@ -115,26 +119,43 @@ def tile_picked_tiegatebharmkindd_none_po_kernel(
         def weave(dst, src, copy):
             copy(dst.rearrange("p (c i) t -> p c t i", i=4), src.rearrange("p t (c i) -> p c t i", i=4))
 
-        def quantise(flat, name):
-            woven = keep.tile([P, S, PACK], BF16, name=name + "_woven", align_bytes=64)
+        def quantise(woven, name):
             codes = keep.tile([P, S], U32, name=name + "_codes", align_bytes=64)
             scales = keep.tile([P, S], U8, name=name + "_scales", align_bytes=64)
-            weave(woven[:], flat[:], nc.vector.tensor_copy)
             nc.vector.quantize_mx(codes[:].bitcast(FP8X4), scales[:], woven[:].rearrange("p c t -> p (c t)"))
             return codes, scales
+
+        ident = keep.tile([P, P], F32, name="ident")
+        make_identity(nc, ident[:])
+
+        def block(j):
+            return slice(j * P, (j + 1) * P)
+
+        def turned_sum(terms, name, bank):
+            acc = psum.tile([P, PACK, P], F32, name=name, tag="bank%d" % bank)
+            for j in range(PACK):
+                for i, term in enumerate(terms):
+                    nc.tensor.matmul(acc[:, j, :], term[:, block(j)], ident[:], start=(i == 0), stop=(i == len(terms) - 1), is_transpose=True)
+            return acc[:].rearrange("c j p -> c (j p)")
+
+        def turned_back(turned, j, name, bank):
+            acc = psum.tile([P, PACK, P], F32, name=name, tag="bank%d" % bank)
+            for t in range(PACK):
+                nc.tensor.transpose(acc[:, t, :], turned[t][:, block(j)], ident[:])
+            return acc
 
         w1 = deal(w1w_raw, w1s_raw, "w1")
         xs = keep.tile([P, S], U8, name="xs", align_bytes=64)
         xw = keep.tile([P, S], U32, name="xw", align_bytes=64)
         nc.vector.tensor_copy(xs[:], xs_raw[:].indirect(offs_t[:]))
         nc.vector.tensor_copy(xw[:], xw_raw[:].indirect(offs_t[:]))
-        y_banks = product(w1, xw, xs, "ya")
+        y_banks = product(w1, xw, xs, "y", 0)
         w2 = deal(w2w_raw, w2s_raw, "w2")
 
         tab_g = planes("tab_g")
         for t in range(PACK):
             for h in range(2):
-                nc.scalar.activation(tab_g[:, t, cols(h)], tab_t[t][:].indirect(half_of(n2_t, h)), ACT.Copy)
+                nc.scalar.activation(tab_g[:, t, cols(h)], tab_t[t][:].indirect(half_of(n2_t, h)), ACT.Copy, scale=-1.0)
 
         gain2 = keep.tile([P, PACK], F32, name="gain2")
         nc.vector.tensor_scalar(gain2[:], gain[:], 2.0, None, ALU.mult)
@@ -146,24 +167,30 @@ def tile_picked_tiegatebharmkindd_none_po_kernel(
             else:
                 nc.vector.tensor_copy(y[t][:], y_banks[t][:])
 
-        both, diff, size = (planes(n) for n in ("both", "diff", "size"))
-        z2 = planes("z2", BF16)
+        y_n3 = planes("y_n3")
+        size = rows("size")
         for t in range(PACK):
             for h in range(2):
-                nc.vector.tensor_tensor(both[:, t, cols(h)], y[t][:].indirect(half_of(n3_t, h)), tab_g[:, t, cols(h)], ALU.add)
-            nc.vector.tensor_tensor(diff[:, t, :], y[t][:], both[:, t, :], ALU.subtract)
-            nc.scalar.activation(size[:, t, :], diff[:, t, :], ACT.Abs)
-        for t in range(PACK):
-            nc.vector.tensor_scalar(z2[:, t, :], size[:, t, :], gain[:, t : t + 1], None, ALU.mult)
+                if t in ():
+                    nc.scalar.activation(y_n3[:, t, cols(h)], y[t][:].indirect(half_of(n3_t, h)), ACT.Copy, scale=-1.0)
+                else:
+                    nc.vector.tensor_scalar(y_n3[:, t, cols(h)], y[t][:].indirect(half_of(n3_t, h)), -1.0, 0.0, ALU.mult, ALU.add)
+            diff = turned_sum([tab_g[:, t, :], y[t][:], y_n3[:, t, :]], "diff%d" % t, 4 + t % 4)
+            nc.scalar.activation(size[t][:], diff, ACT.Abs)
+        z2 = keep.tile([P, S, PACK], BF16, name="z2", align_bytes=64)
+        gain_b = gain[:].unsqueeze(1).to_broadcast([P, P, PACK])
+        for j in range(PACK):
+            back = turned_back(size, j, "size_back%d" % j, j)
+            nc.vector.tensor_tensor(z2[:, block(j), :], back[:].rearrange("p t c -> p c t"), gain_b, ALU.mult)
         z2_codes, z2_scales = quantise(z2, "z2")
-        b_banks = product(w2, z2_codes, z2_scales, "b")
+        b_banks = product(w2, z2_codes, z2_scales, "b", 0)
 
-        pa, y_sq, pa_sq, den, recip, num = (planes(n) for n in ("pa", "y_sq", "pa_sq", "den", "recip", "num"))
-        root = [keep.tile([P, S], F32, name="root%d" % t, tag="root_or_b%d" % t, align_bytes=64) for t in range(PACK)]
-        z = planes("z", BF16)
+        pa, y_sq, pa_sq, num = (planes(n) for n in ("pa", "y_sq", "pa_sq", "num"))
+        root = keep.tile([P, PACK, S], F32, name="root", tag="root_or_gate", align_bytes=64)
+        recip = planes("recip")
         for t in range(PACK):
             for h in range(2):
-                if t in (0,1,2):
+                if t in (0,1):
                     nc.scalar.activation(pa[:, t, cols(h)], y[t][:].indirect(half_of(n1_t, h)), ACT.Copy)
                 else:
                     nc.vector.tensor_copy(pa[:, t, cols(h)], y[t][:].indirect(half_of(n1_t, h)))
@@ -173,50 +200,78 @@ def tile_picked_tiegatebharmkindd_none_po_kernel(
                 nc.gpsimd.tensor_tensor(y_sq[:, t, :], y[t][:], y[t][:], ALU.mult)
             else:
                 nc.scalar.activation(y_sq[:, t, :], y[t][:], ACT.Square)
-            nc.scalar.activation(pa_sq[:, t, :], pa[:, t, :], ACT.Square)
+            if t in ():
+                nc.vector.tensor_tensor(pa_sq[:, t, :], pa[:, t, :], pa[:, t, :], ALU.mult)
+            elif t in ():
+                nc.gpsimd.tensor_tensor(pa_sq[:, t, :], pa[:, t, :], pa[:, t, :], ALU.mult)
+            else:
+                nc.scalar.activation(pa_sq[:, t, :], pa[:, t, :], ACT.Square)
+        den = planes("den")
         for t in range(PACK):
             nc.vector.scalar_tensor_tensor(den[:, t, :], pa_sq[:, t, :], 0.5, y_sq[:, t, :], ALU.add, ALU.add)
         for t in range(PACK):
-            nc.scalar.activation(root[t][:], den[:, t, :], ACT.Abs_reciprocal_sqrt)
-            nc.scalar.activation(recip[:, t, :], root[t][:], ACT.Square)
+            nc.scalar.activation(root[:, t, :], den[:, t, :], ACT.Abs_reciprocal_sqrt)
+            if t in ():
+                nc.vector.tensor_tensor(recip[:, t, :], root[:, t, :], root[:, t, :], ALU.mult)
+            else:
+                nc.scalar.activation(recip[:, t, :], root[:, t, :], ACT.Square)
         for t in range(PACK):
             nc.vector.scalar_tensor_tensor(num[:, t, :], pa[:, t, :], gain2[:, t : t + 1], y[t][:], ALU.mult, ALU.mult)
-            nc.vector.tensor_tensor(z[:, t, :], num[:, t, :], recip[:, t, :], ALU.mult)
+        z = keep.tile([P, S, PACK], BF16, name="z", align_bytes=64)
+        for h in range(2):
+            nc.vector.tensor_tensor(
+                z[:, cols(h), :].rearrange("p (c i) t -> p c t i", i=4),
+                num[:, :, cols(h)].rearrange("p t (c i) -> p c t i", i=4),
+                recip[:, :, cols(h)].rearrange("p t (c i) -> p c t i", i=4),
+                ALU.mult,
+            )
         z_codes, z_scales = quantise(z, "z")
-        a_banks = product(w2, z_codes, z_scales, "ya")
+        a_banks = product(w2, z_codes, z_scales, "a", 4)
 
-        b = [keep.tile([P, S], F32, name="b%d" % t, tag="root_or_b%d" % (PACK - 1 - t), align_bytes=64) for t in range(PACK)]
+        b = rows("b")
         neg_half_a = rows("neg_half_a")
-        gate, gated, result = (planes(n) for n in ("gate", "gated", "result"))
-        out_rows = out_0.rearrange("(p t) j -> t p j", t=PACK)
-        fetched = planes("fetched")
+        gate = keep.tile([P, PACK, S], F32, name="gate", tag="root_or_gate", align_bytes=64)
+        gated = planes("gated")
         for t in range(PACK):
             if t in ():
                 nc.scalar.copy(b[t][:], b_banks[t][:])
             else:
                 nc.vector.tensor_copy(b[t][:], b_banks[t][:])
         for t in range(PACK):
-            nc.scalar.activation(neg_half_a[t][:], a_banks[t][:], ACT.Copy, scale=-0.5)
             for h in range(2):
                 nc.scalar.activation(gate[:, t, cols(h)], b[t][:].indirect(half_of(n5_t, h)), ACT.Sigmoid)
-            nc.vector.scalar_tensor_tensor(gated[:, t, :], gate[:, t, :], -2.0, neg_half_a[t][:], ALU.mult, ALU.mult)
-            if t in (3,):
-                for h in range(2):
-                    nc.scalar.activation(fetched[:, t, cols(h)], neg_half_a[t][:].indirect(half_of(n4_t, h)), ACT.Copy)
-                nc.vector.tensor_tensor(result[:, t, :], fetched[:, t, :], gated[:, t, :], ALU.add)
-            else:
-                for h in range(2):
-                    nc.vector.tensor_tensor(result[:, t, cols(h)], neg_half_a[t][:].indirect(half_of(n4_t, h)), gated[:, t, cols(h)], ALU.add)
-            nc.sync.dma_start(out_rows[t], result[:, t, :])
+        for t in range(PACK):
+            nc.vector.tensor_tensor(gated[:, t, :], a_banks[t][:], gate[:, t, :], ALU.mult)
+            nc.scalar.activation(neg_half_a[t][:], a_banks[t][:], ACT.Copy, scale=-0.5)
 
+        out_rows = out_0.rearrange("(p t) j -> p t j", t=PACK)
         out_codes = keep.tile([P, S], U32, name="out_codes", align_bytes=64)
         out_scales = keep.tile([P, S], U8, name="out_scales", align_bytes=64)
         out_words = out_1[0].rearrange("p c r -> p (c r)").bitcast(I32)
-        split = 320
-        woven = keep.tile([P, S, PACK], BF16, name="out_woven", align_bytes=64)
-        weave(woven[:, :split, :], result[:, :, :split], nc.vector.tensor_copy)
-        weave(woven[:, split:, :], result[:, :, split:], nc.scalar.copy)
-        nc.vector.quantize_mx(out_codes[:].bitcast(FP8X4), out_scales[:], woven[:].rearrange("p c t -> p (c t)"))
-        nc.sync.dma_start(out_words, out_codes[:].bitcast(I32))
+        first = 0
+        chunks = (256, 256)
+        for k, width in enumerate(chunks):
+            span = slice(first, first + width)
+            places = n4_t[:, first // 16 : (first + width) // 16]
+            result = keep.tile([P, PACK, width], F32, name="result%d" % k)
+            fetched = keep.tile([P, PACK, width], F32, name="fetched%d" % k)
+            woven = keep.tile([P, width, PACK], BF16, name="out_woven%d" % k, align_bytes=64)
+            for t in range(PACK):
+                if (k, t) in ((1,2),(1,3)):
+                    nc.scalar.activation(fetched[:, t, :], neg_half_a[t][:].indirect(places), ACT.Copy)
+                    nc.vector.tensor_tensor(result[:, t, :], fetched[:, t, :], gated[:, t, span], ALU.add)
+                else:
+                    nc.vector.tensor_tensor(result[:, t, :], neg_half_a[t][:].indirect(places), gated[:, t, span], ALU.add)
+            nc.sync.dma_start(out_rows[:, :, span], result[:])
+            if k in (0,):
+                weave(woven[:], result[:], nc.scalar.copy)
+            else:
+                split = 160
+                weave(woven[:, :split, :], result[:, :, :split], nc.vector.tensor_copy)
+                if split < width:
+                    weave(woven[:, split:, :], result[:, :, split:], nc.scalar.copy)
+            nc.vector.quantize_mx(out_codes[:, span].bitcast(FP8X4), out_scales[:, span], woven[:].rearrange("p c t -> p (c t)"))
+            nc.sync.dma_start(out_words[:, span], out_codes[:, span].bitcast(I32))
+            first = first + width
         for q in range(4):
-            nc.scalar.dma_start(out_2[0, 4 * q : 4 * q + 4, :].bitcast(I32), out_scales[32 * q : 32 * q + 4, :].bitcast(I32))
+            (nc.scalar if q % 2 else nc.sync).dma_start(out_2[0, 4 * q : 4 * q + 4, :].bitcast(I32), out_scales[32 * q : 32 * q + 4, :].bitcast(I32))

from contextlib import ExitStack

import concourse.mybir as mybir
from concourse.masks import make_identity

F32 = mybir.dt.float32
BF16 = mybir.dt.bfloat16
I32 = mybir.dt.int32
U32 = mybir.dt.uint32
U16 = mybir.dt.uint16
U8 = mybir.dt.uint8
FP8X4 = mybir.dt.float8_e4m3fn_x4
FP4X4 = mybir.dt.float4_e2m1fn_x4
ALU = mybir.AluOpType
ACT = mybir.ActivationFunctionType

P = 128
PACK = 4
T = 2048
S = 512
H = 512
HALF = S // 2
FLOPS = 3 * 2 * 512 * 512 * 512


def tile_picked_tiegatebharmkindd_none_po_kernel(
    tc, x_words, x_scales, w1_words, w1_scales, tab, gn, w2_words, w2_scales, offs, n1, n2, n3, n4, n5, out_0, out_1, out_2
):
    nc = tc.nc
    with ExitStack() as ctx:
        lists = ctx.enter_context(tc.tile_pool(name="lists", bufs=1))
        keep = ctx.enter_context(tc.tile_pool(name="keep", bufs=1))
        psum = ctx.enter_context(tc.psum_pool(name="psum", bufs=1))

        def load_list(src, name):
            tile = lists.tile([P, S // 16], U16, name=name)
            nc.sync.dma_start(tile[:], src)
            return tile

        def half_of(lst, h):
            return lst[:, h * (HALF // 16) : (h + 1) * (HALF // 16)]

        def cols(h):
            return slice(h * HALF, (h + 1) * HALF)

        def load_scale_rows(tile, src):
            for q in range(4):
                nc.sync.dma_start(tile[32 * q : 32 * q + 4, :].bitcast(I32), src[0, 4 * q : 4 * q + 4, :].bitcast(I32))

        def planes(name, dtype=F32):
            return keep.tile([P, PACK, S], dtype, name=name, align_bytes=64)

        def rows(name):
            return [keep.tile([P, S], F32, name="%s%d" % (name, t), align_bytes=64) for t in range(PACK)]

        xs_raw = keep.tile([P, T], U8, name="xs_raw", align_bytes=64)
        w1s_raw = keep.tile([P, H], U8, name="w1s_raw", align_bytes=64)
        w2s_raw = keep.tile([P, H], U8, name="w2s_raw", align_bytes=64)
        for tile in (xs_raw, w1s_raw, w2s_raw):
            nc.vector.memset(tile[:].bitcast(I32), 0)

        xw_raw = keep.tile([P, T], U32, name="xw_raw", align_bytes=64)
        w1w_raw = keep.tile([P, 2 * H], U8, name="w1w_raw", align_bytes=64)
        w2w_raw = keep.tile([P, 2 * H], U8, name="w2w_raw", align_bytes=64)
        tab_t = rows("tab")
        gain = keep.tile([P, PACK], F32, name="gain")

        x_rows = x_words[0].rearrange("p c r -> p (c r)").bitcast(I32)
        tab_rows = tab.rearrange("(p t) j -> t p j", t=PACK)
        offs_t = load_list(offs, "offs_t")
        nc.sync.dma_start(w1w_raw[:].bitcast(I32), w1_words[0].bitcast(I32))
        nc.sync.dma_start(xw_raw[:, : T // 2].bitcast(I32), x_rows[:, : T // 2])
        n2_t = load_list(n2, "n2_t")
        nc.sync.dma_start(tab_t[0][:], tab_rows[0])
        load_scale_rows(xs_raw, x_scales)
        nc.sync.dma_start(xw_raw[:, T // 2 :].bitcast(I32), x_rows[:, T // 2 :])
        load_scale_rows(w1s_raw, w1_scales)
        nc.sync.dma_start(tab_t[1][:], tab_rows[1])
        nc.sync.dma_start(tab_t[2][:], tab_rows[2])
        nc.sync.dma_start(tab_t[3][:], tab_rows[3])
        n3_t = load_list(n3, "n3_t")
        nc.sync.dma_start(w2w_raw[:].bitcast(I32), w2_words[0].bitcast(I32))
        n1_t = load_list(n1, "n1_t")
        nc.sync.dma_start(gain[:], gn.rearrange("(p t) o -> p (t o)", t=PACK))
        load_scale_rows(w2s_raw, w2_scales)
        n5_t = load_list(n5, "n5_t")
        n4_t = load_list(n4, "n4_t")

        def deal(words_raw, scales_raw, name):
            words = keep.tile([P, 2 * H], U8, name=name + "_words", align_bytes=64)
            scales = keep.tile([P, H], U8, name=name + "_scales", align_bytes=64)
            nc.scalar.copy(
                words[:].bitcast(U16).rearrange("p (t m) -> p t m", t=PACK),
                words_raw[:].bitcast(U16).rearrange("p (m t) -> p t m", t=PACK),
            )
            nc.gpsimd.tensor_copy(
                scales[:].rearrange("p (t m) -> p t m", t=PACK),
                scales_raw[:].rearrange("p (m t) -> p t m", t=PACK),
            )
            return words, scales

        def product(weights, codes, scales, name, first):
            words, wscales = weights
            banks = []
            for t in range(PACK):
                bank = psum.tile([P, S], F32, name="%s%d" % (name, t), tag="bank%d" % (first + t))
                nc.tensor.matmul_mx(
                    out=bank[:],
                    lhsT=words[:, 2 * P * t : 2 * P * (t + 1)].bitcast(FP4X4),
                    lhsT_scale=wscales[:, P * t : P * (t + 1)],
                    rhs=codes[:].bitcast(FP8X4),
                    rhs_scale=scales[:],
                    start=True,
                    stop=True,
                )
                banks.append(bank)
            return banks

        def weave(dst, src, copy):
            copy(dst.rearrange("p (c i) t -> p c t i", i=4), src.rearrange("p t (c i) -> p c t i", i=4))

        def quantise(woven, name):
            codes = keep.tile([P, S], U32, name=name + "_codes", align_bytes=64)
            scales = keep.tile([P, S], U8, name=name + "_scales", align_bytes=64)
            nc.vector.quantize_mx(codes[:].bitcast(FP8X4), scales[:], woven[:].rearrange("p c t -> p (c t)"))
            return codes, scales

        ident = keep.tile([P, P], F32, name="ident")
        make_identity(nc, ident[:])

        def block(j):
            return slice(j * P, (j + 1) * P)

        def turned_sum(terms, name, bank):
            acc = psum.tile([P, PACK, P], F32, name=name, tag="bank%d" % bank)
            for j in range(PACK):
                for i, term in enumerate(terms):
                    nc.tensor.matmul(acc[:, j, :], term[:, block(j)], ident[:], start=(i == 0), stop=(i == len(terms) - 1), is_transpose=True)
            return acc[:].rearrange("c j p -> c (j p)")

        def turned_back(turned, j, name, bank):
            acc = psum.tile([P, PACK, P], F32, name=name, tag="bank%d" % bank)
            for t in range(PACK):
                nc.tensor.transpose(acc[:, t, :], turned[t][:, block(j)], ident[:])
            return acc

        w1 = deal(w1w_raw, w1s_raw, "w1")
        xs = keep.tile([P, S], U8, name="xs", align_bytes=64)
        xw = keep.tile([P, S], U32, name="xw", align_bytes=64)
        nc.vector.tensor_copy(xs[:], xs_raw[:].indirect(offs_t[:]))
        nc.vector.tensor_copy(xw[:], xw_raw[:].indirect(offs_t[:]))
        y_banks = product(w1, xw, xs, "y", 0)
        w2 = deal(w2w_raw, w2s_raw, "w2")

        tab_g = planes("tab_g")
        for t in range(PACK):
            for h in range(2):
                nc.scalar.activation(tab_g[:, t, cols(h)], tab_t[t][:].indirect(half_of(n2_t, h)), ACT.Copy, scale=-1.0)

        gain2 = keep.tile([P, PACK], F32, name="gain2")
        nc.vector.tensor_scalar(gain2[:], gain[:], 2.0, None, ALU.mult)

        y = rows("y")
        for t in range(PACK):
            if t in ():
                nc.scalar.copy(y[t][:], y_banks[t][:])
            else:
                nc.vector.tensor_copy(y[t][:], y_banks[t][:])

        y_n3 = planes("y_n3")
        size = rows("size")
        for t in range(PACK):
            for h in range(2):
                if t in ():
                    nc.scalar.activation(y_n3[:, t, cols(h)], y[t][:].indirect(half_of(n3_t, h)), ACT.Copy, scale=-1.0)
                else:
                    nc.vector.tensor_scalar(y_n3[:, t, cols(h)], y[t][:].indirect(half_of(n3_t, h)), -1.0, 0.0, ALU.mult, ALU.add)
            diff = turned_sum([tab_g[:, t, :], y[t][:], y_n3[:, t, :]], "diff%d" % t, 4 + t % 4)
            nc.scalar.activation(size[t][:], diff, ACT.Abs)
        z2 = keep.tile([P, S, PACK], BF16, name="z2", align_bytes=64)
        gain_b = gain[:].unsqueeze(1).to_broadcast([P, P, PACK])
        for j in range(PACK):
            back = turned_back(size, j, "size_back%d" % j, j)
            nc.vector.tensor_tensor(z2[:, block(j), :], back[:].rearrange("p t c -> p c t"), gain_b, ALU.mult)
        z2_codes, z2_scales = quantise(z2, "z2")
        b_banks = product(w2, z2_codes, z2_scales, "b", 0)

        pa, y_sq, pa_sq, num = (planes(n) for n in ("pa", "y_sq", "pa_sq", "num"))
        root = keep.tile([P, PACK, S], F32, name="root", tag="root_or_gate", align_bytes=64)
        recip = planes("recip")
        for t in range(PACK):
            for h in range(2):
                if t in (0,1):
                    nc.scalar.activation(pa[:, t, cols(h)], y[t][:].indirect(half_of(n1_t, h)), ACT.Copy)
                else:
                    nc.vector.tensor_copy(pa[:, t, cols(h)], y[t][:].indirect(half_of(n1_t, h)))
            if t in ():
                nc.vector.tensor_tensor(y_sq[:, t, :], y[t][:], y[t][:], ALU.mult)
            elif t in ():
                nc.gpsimd.tensor_tensor(y_sq[:, t, :], y[t][:], y[t][:], ALU.mult)
            else:
                nc.scalar.activation(y_sq[:, t, :], y[t][:], ACT.Square)
            if t in ():
                nc.vector.tensor_tensor(pa_sq[:, t, :], pa[:, t, :], pa[:, t, :], ALU.mult)
            elif t in ():
                nc.gpsimd.tensor_tensor(pa_sq[:, t, :], pa[:, t, :], pa[:, t, :], ALU.mult)
            else:
                nc.scalar.activation(pa_sq[:, t, :], pa[:, t, :], ACT.Square)
        den = planes("den")
        for t in range(PACK):
            nc.vector.scalar_tensor_tensor(den[:, t, :], pa_sq[:, t, :], 0.5, y_sq[:, t, :], ALU.add, ALU.add)
        for t in range(PACK):
            nc.scalar.activation(root[:, t, :], den[:, t, :], ACT.Abs_reciprocal_sqrt)
            if t in ():
                nc.vector.tensor_tensor(recip[:, t, :], root[:, t, :], root[:, t, :], ALU.mult)
            else:
                nc.scalar.activation(recip[:, t, :], root[:, t, :], ACT.Square)
        for t in range(PACK):
            nc.vector.scalar_tensor_tensor(num[:, t, :], pa[:, t, :], gain2[:, t : t + 1], y[t][:], ALU.mult, ALU.mult)
        z = keep.tile([P, S, PACK], BF16, name="z", align_bytes=64)
        for h in range(2):
            nc.vector.tensor_tensor(
                z[:, cols(h), :].rearrange("p (c i) t -> p c t i", i=4),
                num[:, :, cols(h)].rearrange("p t (c i) -> p c t i", i=4),
                recip[:, :, cols(h)].rearrange("p t (c i) -> p c t i", i=4),
                ALU.mult,
            )
        z_codes, z_scales = quantise(z, "z")
        a_banks = product(w2, z_codes, z_scales, "a", 4)

        b = rows("b")
        neg_half_a = rows("neg_half_a")
        gate = keep.tile([P, PACK, S], F32, name="gate", tag="root_or_gate", align_bytes=64)
        gated = planes("gated")
        for t in range(PACK):
            if t in ():
                nc.scalar.copy(b[t][:], b_banks[t][:])
            else:
                nc.vector.tensor_copy(b[t][:], b_banks[t][:])
        for t in range(PACK):
            for h in range(2):
                nc.scalar.activation(gate[:, t, cols(h)], b[t][:].indirect(half_of(n5_t, h)), ACT.Sigmoid)
        for t in range(PACK):
            nc.vector.tensor_tensor(gated[:, t, :], a_banks[t][:], gate[:, t, :], ALU.mult)
            nc.scalar.activation(neg_half_a[t][:], a_banks[t][:], ACT.Copy, scale=-0.5)

        out_rows = out_0.rearrange("(p t) j -> p t j", t=PACK)
        out_codes = keep.tile([P, S], U32, name="out_codes", align_bytes=64)
        out_scales = keep.tile([P, S], U8, name="out_scales", align_bytes=64)
        out_words = out_1[0].rearrange("p c r -> p (c r)").bitcast(I32)
        first = 0
        chunks = (256, 256)
        for k, width in enumerate(chunks):
            span = slice(first, first + width)
            places = n4_t[:, first // 16 : (first + width) // 16]
            result = keep.tile([P, PACK, width], F32, name="result%d" % k)
            fetched = keep.tile([P, PACK, width], F32, name="fetched%d" % k)
            woven = keep.tile([P, width, PACK], BF16, name="out_woven%d" % k, align_bytes=64)
            for t in range(PACK):
                if (k, t) in ((1,2),(1,3)):
                    nc.scalar.activation(fetched[:, t, :], neg_half_a[t][:].indirect(places), ACT.Copy)
                    nc.vector.tensor_tensor(result[:, t, :], fetched[:, t, :], gated[:, t, span], ALU.add)
                else:
                    nc.vector.tensor_tensor(result[:, t, :], neg_half_a[t][:].indirect(places), gated[:, t, span], ALU.add)
            nc.sync.dma_start(out_rows[:, :, span], result[:])
            if k in (0,):
                weave(woven[:], result[:], nc.scalar.copy)
            else:
                split = 160
                weave(woven[:, :split, :], result[:, :, :split], nc.vector.tensor_copy)
                if split < width:
                    weave(woven[:, split:, :], result[:, :, split:], nc.scalar.copy)
            nc.vector.quantize_mx(out_codes[:, span].bitcast(FP8X4), out_scales[:, span], woven[:].rearrange("p c t -> p (c t)"))
            nc.sync.dma_start(out_words[:, span], out_codes[:, span].bitcast(I32))
            first = first + width
        for q in range(4):
            (nc.scalar if q % 2 else nc.sync).dma_start(out_2[0, 4 * q : 4 * q + 4, :].bitcast(I32), out_scales[32 * q : 32 * q + 4, :].bitcast(I32))
